import numpy as np
import ml_dtypes


def mxq(x, axis, fmt="e4m3"):
    dtype, down = {"e4m3": (ml_dtypes.float8_e4m3fn, 7), "e5m2": (ml_dtypes.float8_e5m2, 14)}[fmt]
    v = np.moveaxis(np.asarray(x, np.float32).astype(ml_dtypes.bfloat16).astype(np.float64), axis, -1)
    blocks = v.reshape(v.shape[:-1] + (-1, 32))
    amax = np.abs(blocks).max(-1, keepdims=True)
    byte = np.maximum(np.where(amax > 0, np.frexp(amax)[1] - 1 + 127, 0) - down, 1)
    scale = np.exp2(byte - 127.0)
    codes = (blocks / scale).astype(np.float32).astype(dtype).astype(np.float64)
    return np.moveaxis((codes * scale).reshape(v.shape), -1, axis)


WIDE = False


def mx_kscale(k):
    if not WIDE:
        return np.ones(k)
    levels = np.array([10, -10, 5, -5, 0])
    if k % 512:
        return np.exp2(np.random.permutation(np.resize(levels, k // 32))).repeat(32)
    a = np.empty((k // 512, 16))
    for p in range(k // 512):
        a[p, :8] = np.random.permutation(np.resize(levels, 8))
        for g in range(8):
            far = levels[np.abs(levels - a[p, g]) >= 10]
            a[p, g + 8] = far[np.random.randint(len(far))]
    return np.exp2(a.ravel()).repeat(32)


def f64(x):
    return np.asarray(x).astype(np.float64)


def striped(idx):
    return np.tile(idx.reshape(-1, 16).T, (8, 1)).astype(np.uint16)


def unstriped(offs):
    return offs[:16].T.reshape(-1).astype(np.int64)


def pack_weight(w):
    k, n = w.shape
    w = f64(np.asarray(w, np.float32).astype(ml_dtypes.bfloat16)).reshape(k // 32, 32, n)
    amax = np.abs(w).max(1)
    byte = np.clip(np.where(amax > 0, np.frexp(amax)[1] - 1 + 127 - 7, 1), 1, 254)
    scaled = (w * np.exp2(127.0 - byte)[:, None, :]).reshape(k, n).astype(np.float32)
    words = np.ascontiguousarray(scaled.reshape(k // 512, 128, 4, n).transpose(0, 1, 3, 2)).astype(ml_dtypes.float8_e4m3fn).view(np.uint8)
    return words, np.ascontiguousarray(byte.astype(np.uint8).reshape(k // 512, 16, n))


def unpack_weight(words, scales):
    g, p, n, _ = words.shape
    vals = np.ascontiguousarray(words).view(ml_dtypes.float8_e4m3fn).astype(np.float64) * np.repeat(np.exp2(scales.astype(np.float64) - 127.0), 8, axis=1)[..., None]
    return vals.transpose(0, 1, 3, 2).reshape(g * 512, n)


def sigmoid(v):
    return 1.0 / (1.0 + np.exp(-np.maximum(v, -700.0)))


K, T, S, N, D = 512, 2048, 512, 256, 3
P = 2 ** 7


def setup_inputs():
    n = np.random.standard_normal
    s = mx_kscale(K)[:, None]
    packed_xT = pack_weight(n((K, T)) * s)
    return {
        "x_words": packed_xT[0],
        "x_scales": packed_xT[1],
        "w1": (n((K, N)) / np.sqrt(K) / s).astype(np.float32),
        "adopt": (np.random.uniform(0.0, 0.7, (N, S))).astype(np.float32),
        "infl": (np.tile(np.random.uniform(0.1, 0.6, (D, 1, S)), (1, P, 1))).astype(np.float32),
        "offs": striped(np.random.permutation(T)[:S]),
        "pos1": striped(np.random.permutation(S)[:S]),
        "pos2": striped(np.random.permutation(S)[:S]),
        "pos3": striped(np.random.permutation(S)[:S]),
    }


def reference(x_words, x_scales, w1, adopt, infl, offs, pos1, pos2, pos3):
    xq = unpack_weight(x_words, x_scales)[:, unstriped(offs)]
    y = mxq(f64(w1), 0, "e4m3").T @ xq
    inn = 0.4 * sigmoid(y)
    hza = -1.0 * ((-1.0 * inn + 1.0) * (np.exp(-1.0 * (f64(adopt)[:, unstriped(pos1)] * f64(infl)[0, :1] + f64(adopt)[:, unstriped(pos2)] * f64(infl)[1, :1] + f64(adopt)[:, unstriped(pos3)] * f64(infl)[2, :1])))) + 1.0
    ada = f64(adopt) + (-1.0 * f64(adopt) + 1.0) * hza
    hzb = -1.0 * ((-1.0 * inn + 1.0) * (np.exp(-1.0 * (ada[:, unstriped(pos1)] * f64(infl)[0, :1] + ada[:, unstriped(pos2)] * f64(infl)[1, :1] + ada[:, unstriped(pos3)] * f64(infl)[2, :1])))) + 1.0
    return (-1.0 * (np.log(-1.0 * (0.98 * hzb) + 1.0))) * (-1.0 * ada + 1.0)

@@ -1,0 +1,194 @@
+from contextlib import ExitStack
+
+import concourse.mybir as mybir
+from concourse.masks import make_identity
+
+K, T, S, N, D = 512, 2048, 512, 256, 3
+P = 128
+PACK = 4
+BLOCKS = N // P
+CHUNKS = S // P
+SPARE = 8
+FLOPS = 2 * K * N * S
+
+F32 = mybir.dt.float32
+BF16 = mybir.dt.bfloat16
+I32 = mybir.dt.int32
+U32 = mybir.dt.uint32
+U16 = mybir.dt.uint16
+U8 = mybir.dt.uint8
+FP8X4 = mybir.dt.float8_e4m3fn_x4
+ACT = mybir.ActivationFunctionType
+ALU = mybir.AluOpType
+
+
+def tile_picked_ybassn_haz_p_kernel(
+    tc, x_words, x_scales, w1, adopt, infl, offs, pos1, pos2, pos3, out
+):
+    nc = tc.nc
+    with ExitStack() as ctx:
+        sb = ctx.enter_context(tc.tile_pool(name="sb", bufs=1))
+        ps = ctx.enter_context(tc.psum_pool(name="ps", bufs=1))
+
+        def tiles(name, count, shape, dtype):
+            return [sb.tile(shape, dtype, name="%s%d" % (name, i), align_bytes=64) for i in range(count)]
+
+        def cols(c):
+            return slice(c * P, (c + 1) * P)
+
+        offs_t = sb.tile([P, S // 16], U16, name="offs_t")
+        pos_t = tiles("pos", D, [P, S // 16], U16)
+        scale_tab = sb.tile([P, T], U8, name="scale_tab", align_bytes=64)
+        word_tab = sb.tile([P, T], U32, name="word_tab", tag="words", align_bytes=64)
+        adopt_t = tiles("adopt", BLOCKS, [P, S], F32)
+        infl_first = sb.tile([P, S], F32, name="infl_first", align_bytes=64)
+        infl_rest = sb.tile([P, D - 1, S], F32, name="infl_rest", align_bytes=64)
+        infl_t = [infl_first[:]] + [infl_rest[:, d, :] for d in range(D - 1)]
+        w_raw = sb.tile([P, PACK, N], F32, name="w_raw", align_bytes=64)
+        left = tiles("left", BLOCKS, [P, S + SPARE], F32)
+        stay = tiles("stay", BLOCKS, [P, S + SPARE], F32)
+        ident = sb.tile([P, P], F32, name="ident", align_bytes=64)
+        one = sb.tile([P, 1], F32, name="one")
+        floor = sb.tile([P, 1], F32, name="floor")
+
+        nc.vector.memset(scale_tab[:].bitcast(I32), 0)
+        make_identity(nc, ident[:])
+        for b in range(BLOCKS):
+            nc.gpsimd.memset(left[b][:, S:], 0.0)
+            nc.gpsimd.memset(stay[b][:, S:], 0.0)
+        nc.gpsimd.memset(one[:], 1.0)
+        nc.gpsimd.tensor_scalar(floor[:], one[:], 0.02, 0.0, ALU.mult, ALU.add)
+
+        for q in range(4):
+            nc.sync.dma_start(
+                scale_tab[32 * q : 32 * q + 4, :].bitcast(I32), x_scales[0, 4 * q : 4 * q + 4, :].bitcast(I32)
+            )
+        nc.sync.dma_start(offs_t[:], offs)
+        nc.sync.dma_start(adopt_t[0][:], adopt[cols(0), :])
+        nc.sync.dma_start(infl_first[:], infl[0])
+        nc.sync.dma_start(pos_t[0][:], pos1)
+        nc.sync.dma_start(infl_rest[:], infl[1:].rearrange("d p s -> p d s"))
+        nc.sync.dma_start(pos_t[1][:], pos2)
+        nc.sync.dma_start(pos_t[2][:], pos3)
+        nc.sync.dma_start(adopt_t[1][:], adopt[cols(1), :])
+        nc.sync.dma_start(w_raw[:], w1.rearrange("(p j) n -> p j n", j=PACK))
+        nc.sync.dma_start(word_tab[:].bitcast(I32), x_words[0].rearrange("p n t -> p (n t)").bitcast(I32))
+
+        x_scale = sb.tile([P, S], U8, name="x_scale", align_bytes=64)
+        x_code = sb.tile([P, S], U32, name="x_code", align_bytes=64)
+        w_bf = sb.tile([P, N, PACK], BF16, name="w_bf", align_bytes=64)
+        w_code = sb.tile([P, N], U32, name="w_code", align_bytes=64)
+        w_scale = sb.tile([P, N], U8, name="w_scale", align_bytes=64)
+        neg_total = sb.tile([P, CHUNKS], F32, name="neg_total")
+        pull = [[t[:] for t in tiles("pull0_", D, [P, S], F32)], [t[:] for t in tiles("pull1_", 1, [P, S], F32)]]
+        push = [tiles("push%d_" % b, D, [P, S], F32) for b in range(BLOCKS)]
+        th = tiles("th", BLOCKS, [P, S], F32)
+        ea_t = tiles("ea_t", BLOCKS, [P, S], F32)
+        eb_t = tiles("eb_t", BLOCKS, [P, S], F32)
+        xq = tiles("xq", BLOCKS, [P, S], F32)
+        res = tiles("res", BLOCKS, [P, S], F32)
+
+        def bank(tag):
+            return ps.tile([P, S], F32, name=tag, tag=tag)
+
+        def add_turned(acc, src, chunks, first, last):
+            for c in chunks:
+                nc.tensor.matmul(
+                    acc[:, cols(c)], src[:, cols(c)], ident[:], is_transpose=True,
+                    start=first and c == chunks[0], stop=last and c == chunks[-1],
+                )
+
+        def exp_turned(acc, staged, chunks, scale):
+            for c in chunks:
+                nc.scalar.activation(
+                    staged[:, cols(c)], acc[:, cols(c)], ACT.Exp, bias=neg_total[:, c : c + 1], scale=scale
+                )
+
+        def turn_back(staged, back):
+            for c in range(CHUNKS):
+                nc.tensor.transpose(back[:, cols(c)], staged[:, cols(c)], ident[:])
+
+        def gather(term, window, d, factor, lo, hi):
+            nc.vector.tensor_tensor(
+                term[:, lo:hi], window[:].indirect(pos_t[d][:, lo // 16 : hi // 16]), factor[:, lo:hi], ALU.mult
+            )
+
+        ALL = list(range(CHUNKS))
+
+        nc.vector.tensor_copy(x_scale[:], scale_tab[:].indirect(offs_t[:]))
+        nc.scalar.activation(left[0][:, :S], adopt_t[0][:], ACT.Copy, bias=1.0, scale=-1.0)
+
+        total = bank("total")
+        for d in range(D):
+            add_turned(total, infl_t[d], ALL, d == 0, d == D - 1)
+        nc.scalar.activation(neg_total[:], total[:, 0:S:P], ACT.Copy, scale=-1.0)
+
+        nc.scalar.activation(left[1][:, :S], adopt_t[1][:], ACT.Copy, bias=1.0, scale=-1.0)
+        nc.scalar.copy(w_bf[:], w_raw[:].rearrange("p j n -> p n j"))
+
+        sum_a = [bank("sum_a%d" % b) for b in range(BLOCKS)]
+        ea = [bank("ea%d" % b) for b in range(BLOCKS)]
+        for d in range(D):
+            gather(pull[0][d], left[0], d, infl_t[d], 0, S)
+            add_turned(sum_a[0], pull[0][d], ALL, d == 0, d == D - 1)
+        exp_turned(sum_a[0], ea_t[0], ALL, 1.0)
+        turn_back(ea_t[0], ea[0])
+        gather(pull[1][0], left[1], 0, infl_t[0], 0, S)
+        add_turned(sum_a[1], pull[1][0], ALL, True, False)
+
+        nc.vector.quantize_mx(w_code[:].bitcast(FP8X4), w_scale[:], w_bf[:].rearrange("p n j -> p (n j)"))
+        nc.vector.tensor_copy(x_code[:], word_tab[:].indirect(offs_t[:]))
+        y = [bank("y%d" % b) for b in range(BLOCKS)]
+        for b in range(BLOCKS):
+            nc.tensor.matmul_mx(
+                y[b][:], lhsT=w_code[:, cols(b)].bitcast(FP8X4), lhsT_scale=w_scale[:, cols(b)],
+                rhs=x_code[:].bitcast(FP8X4), rhs_scale=x_scale[:], start=True, stop=True,
+            )
+            nc.scalar.activation(th[b][:], y[b][:], ACT.Tanh, scale=0.5)
+
+        late = sb.tile([P, D - 1, S], F32, name="late", tag="words", align_bytes=64)
+        pull[1].extend(late[:, d, :] for d in range(D - 1))
+        for d in range(1, D):
+            gather(pull[1][d], left[1], d, infl_t[d], 0, S)
+            add_turned(sum_a[1], pull[1][d], ALL, False, d == D - 1)
+        exp_turned(sum_a[1], ea_t[1], ALL, 1.0)
+        turn_back(ea_t[1], ea[1])
+
+        eb = []
+        nc.vector.scalar_tensor_tensor(stay[0][:, :S], th[0][:], 4.0, ea[0][:], ALU.subtract, ALU.mult)
+        sum_b = bank("sum_a0")
+        eb.append(bank("y0"))
+        for d in range(D):
+            gather(push[0][d], stay[0], d, pull[0][d], 0, S)
+            add_turned(sum_b, push[0][d], ALL, d == 0, d == D - 1)
+        exp_turned(sum_b, eb_t[0], ALL, -0.2)
+        turn_back(eb_t[0], eb[0])
+
+        nc.vector.scalar_tensor_tensor(stay[1][:, :S], th[1][:], 4.0, ea[1][:], ALU.subtract, ALU.mult)
+        halves = [(bank("sum_a1"), ALL[:2]), (bank("total"), ALL[2:])]
+        eb.append(bank("y1"))
+        for d in range(D - 1):
+            gather(push[1][d], stay[1], d, pull[1][d], 0, S)
+            for acc, chunks in halves:
+                add_turned(acc, push[1][d], chunks, d == 0, False)
+        for acc, chunks in halves:
+            gather(push[1][D - 1], stay[1], D - 1, pull[1][D - 1], chunks[0] * P, (chunks[-1] + 1) * P)
+            add_turned(acc, push[1][D - 1], chunks, False, True)
+            exp_turned(acc, eb_t[1], chunks, -0.2)
+        turn_back(eb_t[1], eb[1])
+
+        x0 = pull[1][2]
+        nc.vector.scalar_tensor_tensor(x0[:], th[0][:], 4.0, eb[0][:], ALU.subtract, ALU.mult)
+        nc.vector.scalar_tensor_tensor(th[0][:], left[0][:, :S], 0.2, stay[0][:, :S], ALU.mult, ALU.mult)
+        nc.vector.scalar_tensor_tensor(push[1][1][:], left[1][:, :S], 0.2, stay[1][:, :S], ALU.mult, ALU.mult)
+        nc.vector.scalar_tensor_tensor(xq[1][:], th[1][:], 4.0, eb[1][:], ALU.subtract, ALU.mult)
+        z0 = eb_t[1]
+        nc.scalar.activation(z0[:], x0[:], ACT.Ln, bias=floor[:], scale=-0.196)
+        nc.vector.tensor_tensor(res[0][:], z0[:], th[0][:], ALU.mult)
+        nc.sync.dma_start(out[cols(0), :], res[0][:])
+        z1 = eb_t[0]
+        for h in range(2):
+            half = slice(h * (S // 2), (h + 1) * (S // 2))
+            nc.scalar.activation(z1[:, half], xq[1][:, half], ACT.Ln, bias=floor[:], scale=-0.196)
+            nc.vector.tensor_tensor(res[1][:, half], z1[:, half], push[1][1][:, half], ALU.mult)
+            nc.sync.dma_start(out[cols(1), half], res[1][:, half])

@@ -59,12 +59,12 @@ def tile_picked_ybassn_haz_p_kernel(
         nc.gpsimd.memset(one[:], 1.0)
         nc.gpsimd.tensor_scalar(floor[:], one[:], 0.02, 0.0, ALU.mult, ALU.add)
 
+        nc.scalar.dma_start(adopt_t[0][:], adopt[cols(0), :])
         for q in range(4):
             nc.sync.dma_start(
                 scale_tab[32 * q : 32 * q + 4, :].bitcast(I32), x_scales[0, 4 * q : 4 * q + 4, :].bitcast(I32)
             )
         nc.sync.dma_start(offs_t[:], offs)
-        nc.sync.dma_start(adopt_t[0][:], adopt[cols(0), :])
         nc.sync.dma_start(infl_first[:], infl[0])
         nc.sync.dma_start(pos_t[0][:], pos1)
         nc.sync.dma_start(infl_rest[:], infl[1:].rearrange("d p s -> p d s"))
@@ -79,7 +79,7 @@ def tile_picked_ybassn_haz_p_kernel(
         w_bf = sb.tile([P, N, PACK], BF16, name="w_bf", align_bytes=64)
         w_code = sb.tile([P, N], U32, name="w_code", align_bytes=64)
         w_scale = sb.tile([P, N], U8, name="w_scale", align_bytes=64)
-        neg_total = sb.tile([P, CHUNKS], F32, name="neg_total")
+        neg_total = sb.tile([P, CHUNKS], F32, name="neg_total", tag="bias", align_bytes=64)
         pull = [[t[:] for t in tiles("pull0_", D, [P, S], F32)], [t[:] for t in tiles("pull1_", 1, [P, S], F32)]]
         push = [tiles("push%d_" % b, D, [P, S], F32) for b in range(BLOCKS)]
         th = tiles("th", BLOCKS, [P, S], F32)
@@ -165,16 +165,17 @@ def tile_picked_ybassn_haz_p_kernel(
         turn_back(eb_t[0], eb[0])
 
         nc.vector.scalar_tensor_tensor(stay[1][:, :S], th[1][:], 4.0, ea[1][:], ALU.subtract, ALU.mult)
-        halves = [(bank("sum_a1"), ALL[:2]), (bank("total"), ALL[2:])]
+        banks = [bank(tag) for tag in ("sum_a1", "total", "ea0", "spare")]
         eb.append(bank("y1"))
         for d in range(D - 1):
             gather(push[1][d], stay[1], d, pull[1][d], 0, S)
-            for acc, chunks in halves:
-                add_turned(acc, push[1][d], chunks, d == 0, False)
-        for acc, chunks in halves:
+            for c in ALL:
+                add_turned(banks[c], push[1][d], [c], d == 0, False)
+        for chunks in (ALL[:2], ALL[2:3], ALL[3:]):
             gather(push[1][D - 1], stay[1], D - 1, pull[1][D - 1], chunks[0] * P, (chunks[-1] + 1) * P)
-            add_turned(acc, push[1][D - 1], chunks, False, True)
-            exp_turned(acc, eb_t[1], chunks, -0.2)
+            for c in chunks:
+                add_turned(banks[c], push[1][D - 1], [c], False, True)
+                exp_turned(banks[c], eb_t[1], [c], -0.2)
         turn_back(eb_t[1], eb[1])
 
         x0 = pull[1][2]
@@ -182,13 +183,10 @@ def tile_picked_ybassn_haz_p_kernel(
         nc.vector.scalar_tensor_tensor(th[0][:], left[0][:, :S], 0.2, stay[0][:, :S], ALU.mult, ALU.mult)
         nc.vector.scalar_tensor_tensor(push[1][1][:], left[1][:, :S], 0.2, stay[1][:, :S], ALU.mult, ALU.mult)
         nc.vector.scalar_tensor_tensor(xq[1][:], th[1][:], 4.0, eb[1][:], ALU.subtract, ALU.mult)
-        z0 = eb_t[1]
-        nc.scalar.activation(z0[:], x0[:], ACT.Ln, bias=floor[:], scale=-0.196)
-        nc.vector.tensor_tensor(res[0][:], z0[:], th[0][:], ALU.mult)
-        nc.sync.dma_start(out[cols(0), :], res[0][:])
-        z1 = eb_t[0]
-        for h in range(2):
-            half = slice(h * (S // 2), (h + 1) * (S // 2))
-            nc.scalar.activation(z1[:, half], xq[1][:, half], ACT.Ln, bias=floor[:], scale=-0.196)
-            nc.vector.tensor_tensor(res[1][:, half], z1[:, half], push[1][1][:, half], ALU.mult)
-            nc.sync.dma_start(out[cols(1), half], res[1][:, half])
+        logs = sb.tile([P, BLOCKS, S], F32, name="logs", tag="bias", align_bytes=64)
+        args = [x0, xq[1]]
+        rest = [th[0], push[1][1]]
+        for b, lo, hi in ((0, 0, S // 2), (0, S // 2, S), (1, 0, S // 2), (1, S // 2, S)):
+            nc.scalar.activation(logs[:, b, lo:hi], args[b][:, lo:hi], ACT.Ln, bias=floor[:], scale=-0.196)
+            nc.vector.tensor_tensor(res[b][:, lo:hi], logs[:, b, lo:hi], rest[b][:, lo:hi], ALU.mult)
+            nc.sync.dma_start(out[cols(b), lo:hi], res[b][:, lo:hi])

@@ -6,8 +6,12 @@ from concourse.masks import make_identity
 K, T, S, N, D = 512, 2048, 512, 256, 3
 P = 128
 PACK = 4
+SCALE_ROWS = K // 32
+QUADRANTS = P // 32
+LIST_GROUP = 16
 BLOCKS = N // P
 CHUNKS = S // P
+HALF = S // 2
 SPARE = 8
 FLOPS = 2 * K * N * S
 
@@ -30,163 +34,183 @@ def tile_picked_ybassn_haz_p_kernel(
         sb = ctx.enter_context(tc.tile_pool(name="sb", bufs=1))
         ps = ctx.enter_context(tc.psum_pool(name="ps", bufs=1))
 
-        def tiles(name, count, shape, dtype):
-            return [sb.tile(shape, dtype, name="%s%d" % (name, i), align_bytes=64) for i in range(count)]
+        def tile(name, shape, dtype, tag=None):
+            return sb.tile(shape, dtype, name=name, tag=tag or name, align_bytes=64)
 
-        def cols(c):
+        def tiles(name, count, shape, dtype):
+            return [tile("%s%d" % (name, i), shape, dtype) for i in range(count)]
+
+        def bank(tag):
+            return ps.tile([P, S], F32, name=tag, tag=tag)
+
+        def part(c):
             return slice(c * P, (c + 1) * P)
 
-        offs_t = sb.tile([P, S // 16], U16, name="offs_t")
-        pos_t = tiles("pos", D, [P, S // 16], U16)
-        scale_tab = sb.tile([P, T], U8, name="scale_tab", align_bytes=64)
-        word_tab = sb.tile([P, T], U32, name="word_tab", tag="words", align_bytes=64)
+        offs_t = tile("offs_t", [P, S // LIST_GROUP], U16)
+        pos_t = tiles("pos", D, [P, S // LIST_GROUP], U16)
+        scale_table = tile("scale_table", [P, T], U8)
+        picked_scale = tile("picked_scale", [P, S], U8)
+        word_table = tile("word_table", [P, T], U32)
         adopt_t = tiles("adopt", BLOCKS, [P, S], F32)
-        infl_first = sb.tile([P, S], F32, name="infl_first", align_bytes=64)
-        infl_rest = sb.tile([P, D - 1, S], F32, name="infl_rest", align_bytes=64)
+        infl_first = tile("infl_first", [P, S], F32)
+        infl_rest = tile("infl_rest", [P, D - 1, S], F32)
         infl_t = [infl_first[:]] + [infl_rest[:, d, :] for d in range(D - 1)]
-        w_raw = sb.tile([P, PACK, N], F32, name="w_raw", align_bytes=64)
+        w_raw = tile("w_raw", [P, PACK, N], F32)
         left = tiles("left", BLOCKS, [P, S + SPARE], F32)
         stay = tiles("stay", BLOCKS, [P, S + SPARE], F32)
-        ident = sb.tile([P, P], F32, name="ident", align_bytes=64)
-        one = sb.tile([P, 1], F32, name="one")
-        floor = sb.tile([P, 1], F32, name="floor")
+        ident = tile("ident", [P, P], F32)
+        one = tile("one", [P, 1], F32)
+        log_bias = tile("log_bias", [P, 1], F32)
 
-        nc.vector.memset(scale_tab[:].bitcast(I32), 0)
+        nc.vector.memset(scale_table[:].bitcast(I32), 0)
         make_identity(nc, ident[:])
         for b in range(BLOCKS):
             nc.gpsimd.memset(left[b][:, S:], 0.0)
             nc.gpsimd.memset(stay[b][:, S:], 0.0)
         nc.gpsimd.memset(one[:], 1.0)
-        nc.gpsimd.tensor_scalar(floor[:], one[:], 0.02, 0.0, ALU.mult, ALU.add)
+        nc.gpsimd.tensor_scalar(log_bias[:], one[:], 0.02, 0.0, ALU.mult, ALU.add)
 
-        nc.scalar.dma_start(adopt_t[0][:], adopt[cols(0), :])
-        for q in range(4):
-            nc.sync.dma_start(
-                scale_tab[32 * q : 32 * q + 4, :].bitcast(I32), x_scales[0, 4 * q : 4 * q + 4, :].bitcast(I32)
-            )
+        nc.sync.dma_start(scale_table[0:SCALE_ROWS, :].bitcast(I32), x_scales[0].bitcast(I32))
         nc.sync.dma_start(offs_t[:], offs)
-        nc.sync.dma_start(infl_first[:], infl[0])
         nc.sync.dma_start(pos_t[0][:], pos1)
+        nc.sync.dma_start(adopt_t[0][:], adopt[part(0), :])
+        nc.sync.dma_start(infl_first[:], infl[0])
         nc.sync.dma_start(infl_rest[:], infl[1:].rearrange("d p s -> p d s"))
         nc.sync.dma_start(pos_t[1][:], pos2)
         nc.sync.dma_start(pos_t[2][:], pos3)
-        nc.sync.dma_start(adopt_t[1][:], adopt[cols(1), :])
-        nc.sync.dma_start(w_raw[:], w1.rearrange("(p j) n -> p j n", j=PACK))
-        nc.sync.dma_start(word_tab[:].bitcast(I32), x_words[0].rearrange("p n t -> p (n t)").bitcast(I32))
+        nc.sync.dma_start(adopt_t[1][:], adopt[part(1), :])
+        nc.sync.dma_start(w_raw[:], w1.rearrange("(p t) n -> p t n", t=PACK))
+        nc.sync.dma_start(word_table[:].bitcast(I32), x_words[0].rearrange("p n t -> p (n t)").bitcast(I32))
 
-        x_scale = sb.tile([P, S], U8, name="x_scale", align_bytes=64)
-        x_code = sb.tile([P, S], U32, name="x_code", align_bytes=64)
-        w_bf = sb.tile([P, N, PACK], BF16, name="w_bf", align_bytes=64)
-        w_code = sb.tile([P, N], U32, name="w_code", align_bytes=64)
-        w_scale = sb.tile([P, N], U8, name="w_scale", align_bytes=64)
-        neg_total = sb.tile([P, CHUNKS], F32, name="neg_total", tag="bias", align_bytes=64)
-        pull = [[t[:] for t in tiles("pull0_", D, [P, S], F32)], [t[:] for t in tiles("pull1_", 1, [P, S], F32)]]
-        push = [tiles("push%d_" % b, D, [P, S], F32) for b in range(BLOCKS)]
-        th = tiles("th", BLOCKS, [P, S], F32)
-        ea_t = tiles("ea_t", BLOCKS, [P, S], F32)
-        eb_t = tiles("eb_t", BLOCKS, [P, S], F32)
-        xq = tiles("xq", BLOCKS, [P, S], F32)
-        res = tiles("res", BLOCKS, [P, S], F32)
+        x_code = tile("x_code", [P, S], U32)
+        w_bf = tile("w_bf", [P, N, PACK], BF16)
+        w_code = tile("w_code", [P, N], U32)
+        w_scale = tile("w_scale", [P, N], U8)
+        neg_total = tile("neg_total", [P, CHUNKS], F32)
+        tanh_y = tiles("tanh_y", BLOCKS, [P, S], F32)
+        e1_turned = tiles("e1_turned", BLOCKS, [P, S], F32)
+        e2_turned = tiles("e2_turned", BLOCKS, [P, S], F32)
+        every = list(range(CHUNKS))
 
-        def bank(tag):
-            return ps.tile([P, S], F32, name=tag, tag=tag)
-
-        def add_turned(acc, src, chunks, first, last):
+        def add_turned(acc, src, chunks, opens, closes):
             for c in chunks:
                 nc.tensor.matmul(
-                    acc[:, cols(c)], src[:, cols(c)], ident[:], is_transpose=True,
-                    start=first and c == chunks[0], stop=last and c == chunks[-1],
+                    acc[:, part(c)], src[:, part(c - chunks[0])], ident[:], is_transpose=True,
+                    start=opens and c == chunks[0], stop=closes and c == chunks[-1],
                 )
 
-        def exp_turned(acc, staged, chunks, scale):
+        def exp_turned(acc, turned, chunks, scale):
             for c in chunks:
                 nc.scalar.activation(
-                    staged[:, cols(c)], acc[:, cols(c)], ACT.Exp, bias=neg_total[:, c : c + 1], scale=scale
+                    turned[:, part(c)], acc[:, part(c)], ACT.Exp, bias=neg_total[:, c : c + 1], scale=scale
                 )
 
-        def turn_back(staged, back):
-            for c in range(CHUNKS):
-                nc.tensor.transpose(back[:, cols(c)], staged[:, cols(c)], ident[:])
+        def turn_back(turned, dst):
+            for c in every:
+                nc.tensor.transpose(dst[:, part(c)], turned[:, part(c)], ident[:])
 
         def gather(term, window, d, factor, lo, hi):
-            nc.vector.tensor_tensor(
-                term[:, lo:hi], window[:].indirect(pos_t[d][:, lo // 16 : hi // 16]), factor[:, lo:hi], ALU.mult
-            )
+            entries = pos_t[d][:, lo // LIST_GROUP : hi // LIST_GROUP]
+            nc.vector.tensor_tensor(term, window[:].indirect(entries), factor, ALU.mult)
 
-        ALL = list(range(CHUNKS))
+        def times_tanh_less_four(dst, b, e):
+            nc.vector.scalar_tensor_tensor(dst, tanh_y[b][:], 4.0, e[:], ALU.subtract, ALU.mult)
 
-        nc.vector.tensor_copy(x_scale[:], scale_tab[:].indirect(offs_t[:]))
+        nc.vector.tensor_copy(picked_scale[:], scale_table[:].indirect(offs_t[:]))
         nc.scalar.activation(left[0][:, :S], adopt_t[0][:], ACT.Copy, bias=1.0, scale=-1.0)
+
+        x_scale = tile("x_scale", [P, S], U8, tag="adopt0")
+        nc.gpsimd.memset(x_scale[:].bitcast(I32), 0)
+        for q in range(QUADRANTS):
+            nc.sync.dma_start(
+                x_scale[32 * q : 32 * q + 4, :].bitcast(I32), picked_scale[4 * q : 4 * q + 4, :].bitcast(I32)
+            )
 
         total = bank("total")
         for d in range(D):
-            add_turned(total, infl_t[d], ALL, d == 0, d == D - 1)
+            add_turned(total, infl_t[d], every, d == 0, d == D - 1)
         nc.scalar.activation(neg_total[:], total[:, 0:S:P], ACT.Copy, scale=-1.0)
 
         nc.scalar.activation(left[1][:, :S], adopt_t[1][:], ACT.Copy, bias=1.0, scale=-1.0)
-        nc.scalar.copy(w_bf[:], w_raw[:].rearrange("p j n -> p n j"))
+        nc.scalar.copy(w_bf[:], w_raw[:].rearrange("p t n -> p n t"))
 
-        sum_a = [bank("sum_a%d" % b) for b in range(BLOCKS)]
-        ea = [bank("ea%d" % b) for b in range(BLOCKS)]
+        e1 = [bank("e1_%d" % b) for b in range(BLOCKS)]
+        pull0 = tiles("pull0_", D, [P, S], F32)
+        sum1 = bank("sum1_0")
         for d in range(D):
-            gather(pull[0][d], left[0], d, infl_t[d], 0, S)
-            add_turned(sum_a[0], pull[0][d], ALL, d == 0, d == D - 1)
-        exp_turned(sum_a[0], ea_t[0], ALL, 1.0)
-        turn_back(ea_t[0], ea[0])
-        gather(pull[1][0], left[1], 0, infl_t[0], 0, S)
-        add_turned(sum_a[1], pull[1][0], ALL, True, False)
+            gather(pull0[d][:], left[0], d, infl_t[d], 0, S)
+            add_turned(sum1, pull0[d], every, d == 0, d == D - 1)
+        exp_turned(sum1, e1_turned[0], every, 1.0)
+        turn_back(e1_turned[0], e1[0])
+        pull1_first = tile("pull1_first", [P, S], F32)
+        gather(pull1_first[:], left[1], 0, infl_t[0], 0, S)
 
-        nc.vector.quantize_mx(w_code[:].bitcast(FP8X4), w_scale[:], w_bf[:].rearrange("p n j -> p (n j)"))
-        nc.vector.tensor_copy(x_code[:], word_tab[:].indirect(offs_t[:]))
-        y = [bank("y%d" % b) for b in range(BLOCKS)]
+        nc.vector.quantize_mx(w_code[:].bitcast(FP8X4), w_scale[:], w_bf[:].rearrange("p n t -> p (n t)"))
+        nc.vector.tensor_copy(x_code[:], word_table[:].indirect(offs_t[:]))
         for b in range(BLOCKS):
+            y = bank("y%d" % b)
             nc.tensor.matmul_mx(
-                y[b][:], lhsT=w_code[:, cols(b)].bitcast(FP8X4), lhsT_scale=w_scale[:, cols(b)],
+                y[:], lhsT=w_code[:, part(b)].bitcast(FP8X4), lhsT_scale=w_scale[:, part(b)],
                 rhs=x_code[:].bitcast(FP8X4), rhs_scale=x_scale[:], start=True, stop=True,
             )
-            nc.scalar.activation(th[b][:], y[b][:], ACT.Tanh, scale=0.5)
+            nc.scalar.activation(tanh_y[b][:], y[:], ACT.Tanh, scale=0.5)
 
-        late = sb.tile([P, D - 1, S], F32, name="late", tag="words", align_bytes=64)
-        pull[1].extend(late[:, d, :] for d in range(D - 1))
+        sum1 = bank("y1")
+        pull1_rest = tile("pull1_rest", [P, D - 1, S], F32, tag="picked_scale")
+        pull1 = [pull1_first[:]] + [pull1_rest[:, d, :] for d in range(D - 1)]
+        add_turned(sum1, pull1[0], every, True, False)
         for d in range(1, D):
-            gather(pull[1][d], left[1], d, infl_t[d], 0, S)
-            add_turned(sum_a[1], pull[1][d], ALL, False, d == D - 1)
-        exp_turned(sum_a[1], ea_t[1], ALL, 1.0)
-        turn_back(ea_t[1], ea[1])
+            gather(pull1[d], left[1], d, infl_t[d], 0, S)
+            add_turned(sum1, pull1[d], every, False, d == D - 1)
+        exp_turned(sum1, e1_turned[1], every, 1.0)
+        turn_back(e1_turned[1], e1[1])
 
-        eb = []
-        nc.vector.scalar_tensor_tensor(stay[0][:, :S], th[0][:], 4.0, ea[0][:], ALU.subtract, ALU.mult)
-        sum_b = bank("sum_a0")
-        eb.append(bank("y0"))
-        for d in range(D):
-            gather(push[0][d], stay[0], d, pull[0][d], 0, S)
-            add_turned(sum_b, push[0][d], ALL, d == 0, d == D - 1)
-        exp_turned(sum_b, eb_t[0], ALL, -0.2)
-        turn_back(eb_t[0], eb[0])
+        times_tanh_less_four(stay[0][:, :S], 0, e1[0])
+        sum2 = bank("y1")
+        e2 = [bank("sum1_0"), bank("e2_1")]
+        last = D - 1
+        for d in range(last):
+            push = tile("push0_%d" % d, [P, S], F32)
+            gather(push[:], stay[0], d, pull0[d][:], 0, S)
+            add_turned(sum2, push, every, d == 0, False)
+        push = tile("push0_low", [P, HALF], F32)
+        gather(push[:], stay[0], last, pull0[last][:, :HALF], 0, HALF)
+        add_turned(sum2, push, every[: CHUNKS // 2], False, False)
+        times_tanh_less_four(stay[1][:, :S], 1, e1[1])
+        push = tile("push0_high", [P, HALF], F32, tag="e1_turned1")
+        gather(push[:], stay[0], last, pull0[last][:, HALF:], HALF, S)
+        add_turned(sum2, push, every[CHUNKS // 2 :], False, True)
+        exp_turned(sum2, e2_turned[0], every, -0.2)
+        turn_back(e2_turned[0], e2[0])
 
-        nc.vector.scalar_tensor_tensor(stay[1][:, :S], th[1][:], 4.0, ea[1][:], ALU.subtract, ALU.mult)
-        banks = [bank(tag) for tag in ("sum_a1", "total", "ea0", "spare")]
-        eb.append(bank("y1"))
-        for d in range(D - 1):
-            gather(push[1][d], stay[1], d, pull[1][d], 0, S)
-            for c in ALL:
-                add_turned(banks[c], push[1][d], [c], d == 0, False)
-        for chunks in (ALL[:2], ALL[2:3], ALL[3:]):
-            gather(push[1][D - 1], stay[1], D - 1, pull[1][D - 1], chunks[0] * P, (chunks[-1] + 1) * P)
+        sums2 = [bank(tag) for tag in ("y0", "total", "e1_0", "sum2_3")]
+        for d in range(last):
+            push = tile("push1_%d" % d, [P, S], F32)
+            gather(push[:], stay[1], d, pull1[d], 0, S)
+            for c in every:
+                add_turned(sums2[c], push[:, part(c)], [c], d == 0, False)
+        push = tile("push1_last", [P, S], F32)
+        for chunks in (every[:2], every[2:3], every[3:]):
+            lo, hi = chunks[0] * P, (chunks[-1] + 1) * P
+            gather(push[:, lo:hi], stay[1], last, pull1[last][:, lo:hi], lo, hi)
             for c in chunks:
-                add_turned(banks[c], push[1][D - 1], [c], False, True)
-                exp_turned(banks[c], eb_t[1], [c], -0.2)
-        turn_back(eb_t[1], eb[1])
+                add_turned(sums2[c], push[:, part(c)], [c], False, True)
+                exp_turned(sums2[c], e2_turned[1], [c], -0.2)
+        turn_back(e2_turned[1], e2[1])
 
-        x0 = pull[1][2]
-        nc.vector.scalar_tensor_tensor(x0[:], th[0][:], 4.0, eb[0][:], ALU.subtract, ALU.mult)
-        nc.vector.scalar_tensor_tensor(th[0][:], left[0][:, :S], 0.2, stay[0][:, :S], ALU.mult, ALU.mult)
-        nc.vector.scalar_tensor_tensor(push[1][1][:], left[1][:, :S], 0.2, stay[1][:, :S], ALU.mult, ALU.mult)
-        nc.vector.scalar_tensor_tensor(xq[1][:], th[1][:], 4.0, eb[1][:], ALU.subtract, ALU.mult)
-        logs = sb.tile([P, BLOCKS, S], F32, name="logs", tag="bias", align_bytes=64)
-        args = [x0, xq[1]]
-        rest = [th[0], push[1][1]]
-        for b, lo, hi in ((0, 0, S // 2), (0, S // 2, S), (1, 0, S // 2), (1, S // 2, S)):
-            nc.scalar.activation(logs[:, b, lo:hi], args[b][:, lo:hi], ACT.Ln, bias=floor[:], scale=-0.196)
-            nc.vector.tensor_tensor(res[b][:, lo:hi], logs[:, b, lo:hi], rest[b][:, lo:hi], ALU.mult)
-            nc.sync.dma_start(out[cols(b), lo:hi], res[b][:, lo:hi])
+        after_gathers = tile("after_gathers", [P, 1 + BLOCKS, S], F32, tag="picked_scale")
+        log_in = [after_gathers[:, 0, :], tile("log_in1", [P, S], F32)[:]]
+        neg_left2 = [after_gathers[:, 1 + b, :] for b in range(BLOCKS)]
+        times_tanh_less_four(log_in[0], 0, e2[0])
+        for b in range(BLOCKS):
+            nc.vector.scalar_tensor_tensor(neg_left2[b], left[b][:, :S], 0.2, stay[b][:, :S], ALU.mult, ALU.mult)
+        times_tanh_less_four(log_in[1], 1, e2[1])
+
+        logs = tile("logs", [P, BLOCKS, S], F32, tag="neg_total")
+        result = tiles("result", BLOCKS, [P, S], F32)
+        for b in range(BLOCKS):
+            for lo in range(0, S, HALF):
+                half = slice(lo, lo + HALF)
+                nc.scalar.activation(logs[:, b, half], log_in[b][:, half], ACT.Ln, bias=log_bias[:], scale=-0.196)
+                nc.vector.tensor_tensor(result[b][:, half], logs[:, b, half], neg_left2[b][:, half], ALU.mult)
+                nc.sync.dma_start(out[part(b), half], result[b][:, half])

from contextlib import ExitStack

import concourse.mybir as mybir
from concourse.masks import make_identity

K, T, S, N, D = 512, 2048, 512, 256, 3
P = 128
PACK = 4
SCALE_ROWS = K // 32
QUADRANTS = P // 32
LIST_GROUP = 16
BLOCKS = N // P
CHUNKS = S // P
HALF = S // 2
SPARE = 8
FLOPS = 2 * K * N * S

F32 = mybir.dt.float32
BF16 = mybir.dt.bfloat16
I32 = mybir.dt.int32
U32 = mybir.dt.uint32
U16 = mybir.dt.uint16
U8 = mybir.dt.uint8
FP8X4 = mybir.dt.float8_e4m3fn_x4
ACT = mybir.ActivationFunctionType
ALU = mybir.AluOpType


def tile_picked_ybassn_haz_p_kernel(
    tc, x_words, x_scales, w1, adopt, infl, offs, pos1, pos2, pos3, out
):
    nc = tc.nc
    with ExitStack() as ctx:
        sb = ctx.enter_context(tc.tile_pool(name="sb", bufs=1))
        ps = ctx.enter_context(tc.psum_pool(name="ps", bufs=1))

        def tile(name, shape, dtype, tag=None):
            return sb.tile(shape, dtype, name=name, tag=tag or name, align_bytes=64)

        def tiles(name, count, shape, dtype):
            return [tile("%s%d" % (name, i), shape, dtype) for i in range(count)]

        def bank(tag):
            return ps.tile([P, S], F32, name=tag, tag=tag)

        def part(c):
            return slice(c * P, (c + 1) * P)

        offs_t = tile("offs_t", [P, S // LIST_GROUP], U16)
        pos_t = tiles("pos", D, [P, S // LIST_GROUP], U16)
        scale_table = tile("scale_table", [P, T], U8)
        picked_scale = tile("picked_scale", [P, S], U8)
        word_table = tile("word_table", [P, T], U32)
        adopt_t = tiles("adopt", BLOCKS, [P, S], F32)
        infl_first = tile("infl_first", [P, S], F32)
        infl_rest = tile("infl_rest", [P, D - 1, S], F32)
        infl_t = [infl_first[:]] + [infl_rest[:, d, :] for d in range(D - 1)]
        w_raw = tile("w_raw", [P, PACK, N], F32)
        left = tiles("left", BLOCKS, [P, S + SPARE], F32)
        stay = tiles("stay", BLOCKS, [P, S + SPARE], F32)
        ident = tile("ident", [P, P], F32)
        one = tile("one", [P, 1], F32)
        log_bias = tile("log_bias", [P, 1], F32)

        nc.vector.memset(scale_table[:].bitcast(I32), 0)
        make_identity(nc, ident[:])
        for b in range(BLOCKS):
            nc.gpsimd.memset(left[b][:, S:], 0.0)
            nc.gpsimd.memset(stay[b][:, S:], 0.0)
        nc.gpsimd.memset(one[:], 1.0)
        nc.gpsimd.tensor_scalar(log_bias[:], one[:], 0.02, 0.0, ALU.mult, ALU.add)

        nc.sync.dma_start(scale_table[0:SCALE_ROWS, :].bitcast(I32), x_scales[0].bitcast(I32))
        nc.sync.dma_start(offs_t[:], offs)
        nc.sync.dma_start(pos_t[0][:], pos1)
        nc.sync.dma_start(adopt_t[0][:], adopt[part(0), :])
        nc.sync.dma_start(infl_first[:], infl[0])
        nc.sync.dma_start(infl_rest[:], infl[1:].rearrange("d p s -> p d s"))
        nc.sync.dma_start(pos_t[1][:], pos2)
        nc.sync.dma_start(pos_t[2][:], pos3)
        nc.sync.dma_start(adopt_t[1][:], adopt[part(1), :])
        nc.sync.dma_start(w_raw[:], w1.rearrange("(p t) n -> p t n", t=PACK))
        nc.sync.dma_start(word_table[:].bitcast(I32), x_words[0].rearrange("p n t -> p (n t)").bitcast(I32))

        x_code = tile("x_code", [P, S], U32)
        w_bf = tile("w_bf", [P, N, PACK], BF16)
        w_code = tile("w_code", [P, N], U32)
        w_scale = tile("w_scale", [P, N], U8)
        neg_total = tile("neg_total", [P, CHUNKS], F32)
        tanh_y = tiles("tanh_y", BLOCKS, [P, S], F32)
        e1_turned = tiles("e1_turned", BLOCKS, [P, S], F32)
        e2_turned = tiles("e2_turned", BLOCKS, [P, S], F32)
        every = list(range(CHUNKS))

        def add_turned(acc, src, chunks, opens, closes):
            for c in chunks:
                nc.tensor.matmul(
                    acc[:, part(c)], src[:, part(c - chunks[0])], ident[:], is_transpose=True,
                    start=opens and c == chunks[0], stop=closes and c == chunks[-1],
                )

        def exp_turned(acc, turned, chunks, scale):
            for c in chunks:
                nc.scalar.activation(
                    turned[:, part(c)], acc[:, part(c)], ACT.Exp, bias=neg_total[:, c : c + 1], scale=scale
                )

        def turn_back(turned, dst):
            for c in every:
                nc.tensor.transpose(dst[:, part(c)], turned[:, part(c)], ident[:])

        def gather(term, window, d, factor, lo, hi):
            entries = pos_t[d][:, lo // LIST_GROUP : hi // LIST_GROUP]
            nc.vector.tensor_tensor(term, window[:].indirect(entries), factor, ALU.mult)

        def times_tanh_less_four(dst, b, e):
            nc.vector.scalar_tensor_tensor(dst, tanh_y[b][:], 4.0, e[:], ALU.subtract, ALU.mult)

        nc.vector.tensor_copy(picked_scale[:], scale_table[:].indirect(offs_t[:]))
        nc.scalar.activation(left[0][:, :S], adopt_t[0][:], ACT.Copy, bias=1.0, scale=-1.0)

        x_scale = tile("x_scale", [P, S], U8, tag="adopt0")
        nc.gpsimd.memset(x_scale[:].bitcast(I32), 0)
        for q in range(QUADRANTS):
            nc.sync.dma_start(
                x_scale[32 * q : 32 * q + 4, :].bitcast(I32), picked_scale[4 * q : 4 * q + 4, :].bitcast(I32)
            )

        total = bank("total")
        for d in range(D):
            add_turned(total, infl_t[d], every, d == 0, d == D - 1)
        nc.scalar.activation(neg_total[:], total[:, 0:S:P], ACT.Copy, scale=-1.0)

        nc.scalar.activation(left[1][:, :S], adopt_t[1][:], ACT.Copy, bias=1.0, scale=-1.0)
        nc.scalar.copy(w_bf[:], w_raw[:].rearrange("p t n -> p n t"))

        e1 = [bank("e1_%d" % b) for b in range(BLOCKS)]
        pull0 = tiles("pull0_", D, [P, S], F32)
        sum1 = bank("sum1_0")
        for d in range(D):
            gather(pull0[d][:], left[0], d, infl_t[d], 0, S)
            add_turned(sum1, pull0[d], every, d == 0, d == D - 1)
        exp_turned(sum1, e1_turned[0], every, 1.0)
        turn_back(e1_turned[0], e1[0])
        pull1_first = tile("pull1_first", [P, S], F32)
        gather(pull1_first[:], left[1], 0, infl_t[0], 0, S)

        nc.vector.quantize_mx(w_code[:].bitcast(FP8X4), w_scale[:], w_bf[:].rearrange("p n t -> p (n t)"))
        nc.vector.tensor_copy(x_code[:], word_table[:].indirect(offs_t[:]))
        for b in range(BLOCKS):
            y = bank("y%d" % b)
            nc.tensor.matmul_mx(
                y[:], lhsT=w_code[:, part(b)].bitcast(FP8X4), lhsT_scale=w_scale[:, part(b)],
                rhs=x_code[:].bitcast(FP8X4), rhs_scale=x_scale[:], start=True, stop=True,
            )
            nc.scalar.activation(tanh_y[b][:], y[:], ACT.Tanh, scale=0.5)

        sum1 = bank("y1")
        pull1_rest = tile("pull1_rest", [P, D - 1, S], F32, tag="picked_scale")
        pull1 = [pull1_first[:]] + [pull1_rest[:, d, :] for d in range(D - 1)]
        add_turned(sum1, pull1[0], every, True, False)
        for d in range(1, D):
            gather(pull1[d], left[1], d, infl_t[d], 0, S)
            add_turned(sum1, pull1[d], every, False, d == D - 1)
        exp_turned(sum1, e1_turned[1], every, 1.0)
        turn_back(e1_turned[1], e1[1])

        times_tanh_less_four(stay[0][:, :S], 0, e1[0])
        sum2 = bank("y1")
        e2 = [bank("sum1_0"), bank("e2_1")]
        last = D - 1
        for d in range(last):
            push = tile("push0_%d" % d, [P, S], F32)
            gather(push[:], stay[0], d, pull0[d][:], 0, S)
            add_turned(sum2, push, every, d == 0, False)
        push = tile("push0_low", [P, HALF], F32)
        gather(push[:], stay[0], last, pull0[last][:, :HALF], 0, HALF)
        add_turned(sum2, push, every[: CHUNKS // 2], False, False)
        times_tanh_less_four(stay[1][:, :S], 1, e1[1])
        push = tile("push0_high", [P, HALF], F32, tag="e1_turned1")
        gather(push[:], stay[0], last, pull0[last][:, HALF:], HALF, S)
        add_turned(sum2, push, every[CHUNKS // 2 :], False, True)
        exp_turned(sum2, e2_turned[0], every, -0.2)
        turn_back(e2_turned[0], e2[0])

        sums2 = [bank(tag) for tag in ("y0", "total", "e1_0", "sum2_3")]
        for d in range(last):
            push = tile("push1_%d" % d, [P, S], F32)
            gather(push[:], stay[1], d, pull1[d], 0, S)
            for c in every:
                add_turned(sums2[c], push[:, part(c)], [c], d == 0, False)
        push = tile("push1_last", [P, S], F32)
        for chunks in (every[:2], every[2:3], every[3:]):
            lo, hi = chunks[0] * P, (chunks[-1] + 1) * P
            gather(push[:, lo:hi], stay[1], last, pull1[last][:, lo:hi], lo, hi)
            for c in chunks:
                add_turned(sums2[c], push[:, part(c)], [c], False, True)
                exp_turned(sums2[c], e2_turned[1], [c], -0.2)
        turn_back(e2_turned[1], e2[1])

        after_gathers = tile("after_gathers", [P, 1 + BLOCKS, S], F32, tag="picked_scale")
        log_in = [after_gathers[:, 0, :], tile("log_in1", [P, S], F32)[:]]
        neg_left2 = [after_gathers[:, 1 + b, :] for b in range(BLOCKS)]
        times_tanh_less_four(log_in[0], 0, e2[0])
        for b in range(BLOCKS):
            nc.vector.scalar_tensor_tensor(neg_left2[b], left[b][:, :S], 0.2, stay[b][:, :S], ALU.mult, ALU.mult)
        times_tanh_less_four(log_in[1], 1, e2[1])

        logs = tile("logs", [P, BLOCKS, S], F32, tag="neg_total")
        result = tiles("result", BLOCKS, [P, S], F32)
        for b in range(BLOCKS):
            for lo in range(0, S, HALF):
                half = slice(lo, lo + HALF)
                nc.scalar.activation(logs[:, b, half], log_in[b][:, half], ACT.Ln, bias=log_bias[:], scale=-0.196)
                nc.vector.tensor_tensor(result[b][:, half], logs[:, b, half], neg_left2[b][:, half], ALU.mult)
                nc.sync.dma_start(out[part(b), half], result[b][:, half])
